import numpy as np
import ml_dtypes


def mxq(x, axis, fmt="e4m3"):
    dtype, down = {"e4m3": (ml_dtypes.float8_e4m3fn, 7), "e5m2": (ml_dtypes.float8_e5m2, 14)}[fmt]
    v = np.moveaxis(np.asarray(x, np.float32).astype(ml_dtypes.bfloat16).astype(np.float64), axis, -1)
    blocks = v.reshape(v.shape[:-1] + (-1, 32))
    amax = np.abs(blocks).max(-1, keepdims=True)
    byte = np.maximum(np.where(amax > 0, np.frexp(amax)[1] - 1 + 127, 0) - down, 1)
    scale = np.exp2(byte - 127.0)
    codes = (blocks / scale).astype(np.float32).astype(dtype).astype(np.float64)
    return np.moveaxis((codes * scale).reshape(v.shape), -1, axis)


WIDE = False


def mx_kscale(k):
    if not WIDE:
        return np.ones(k)
    levels = np.array([30, -30])
    if k % 512:
        return np.exp2(np.random.permutation(np.resize(levels, k // 32))).repeat(32)
    a = np.empty((k // 512, 16))
    for p in range(k // 512):
        a[p, :8] = np.random.permutation(np.resize(levels, 8))
        for g in range(8):
            far = levels[np.abs(levels - a[p, g]) >= 10]
            a[p, g + 8] = far[np.random.randint(len(far))]
    return np.exp2(a.ravel()).repeat(32)


BF16 = ml_dtypes.bfloat16


def bf(x):
    return np.asarray(x, np.float32).astype(BF16)


def f64(x):
    return np.asarray(x).astype(np.float64)


M, D, F, C = 1024, 1024, 1536, 512


def setup_inputs():
    s, t = mx_kscale(D), mx_kscale(F)
    return {"x": bf(np.random.standard_normal((M, D)) * s),
            "omega": bf(np.random.standard_normal((D, F)) / np.sqrt(D) / s[:, None]),
            "bandwidth": bf(1 + 0.1 * np.random.standard_normal(M)),
            "phase": bf(0.4 * np.random.standard_normal(F)),
            "amp": bf((1 + 0.1 * np.random.standard_normal(F)) * t),
            "w_cos": bf(np.random.standard_normal((F, C)) / np.sqrt(F) / t[:, None]),
            "w_sin": bf(np.random.standard_normal((F, C)) / np.sqrt(F) / t[:, None]),
            "offset_re": bf(0.3 * np.random.standard_normal(C)),
            "offset_im": bf(0.3 * np.random.standard_normal(C))}


def reference(x, omega, bandwidth, phase, amp, w_cos, w_sin, offset_re, offset_im):
    proj = mxq(f64(x), 1, "e4m3") @ mxq(f64(omega), 0, "e4m3")
    z = proj * f64(bandwidth)[:, None] + f64(phase)
    fc = mxq(np.cos(z) * f64(amp), 1, "e5m2")
    fs = mxq(np.sin(z) * f64(amp), 1, "e5m2")
    wc = mxq(f64(w_cos), 0, "e4m3")
    ws = mxq(f64(w_sin), 0, "e4m3")
    re = (fc @ wc) + (fs @ ws) + f64(offset_re)
    im = (fs @ wc) - (fc @ ws) + f64(offset_im)
    return re, im

@@ -1,0 +1,392 @@
+import math
+from contextlib import ExitStack
+
+import concourse.mybir as mybir
+from concourse.masks import make_identity
+
+M, D, F, C = 1024, 1024, 1536, 512
+FLOPS = 2 * M * D * F + 4 * 2 * M * F * C
+
+F32 = mybir.dt.float32
+BF16 = mybir.dt.bfloat16
+I32 = mybir.dt.int32
+U32 = mybir.dt.uint32
+U8 = mybir.dt.uint8
+E4 = mybir.dt.float8_e4m3fn_x4
+E5 = mybir.dt.float8_e5m2_x4
+AF = mybir.ActivationFunctionType
+ALU = mybir.AluOpType
+
+P = 128
+KP = 512
+A = D // KP
+G = F // KP
+W = 256
+NC = M // W
+MT = W // P
+TPB = 512 // W
+TWO_PI = 2.0 * math.pi
+N_GP = 3
+
+
+def tile_complex_fourier_regression_f3_kernel(
+    tc, x, omega, bandwidth, phase, amp, w_cos, w_sin, offset_re, offset_im, out_re, out_im
+):
+    nc = tc.nc
+    with ExitStack() as ctx:
+        keep = ctx.enter_context(tc.tile_pool(name="keep", bufs=1))
+        stage = ctx.enter_context(tc.tile_pool(name="stage", bufs=2))
+        work = ctx.enter_context(tc.tile_pool(name="work", bufs=2))
+        psz = ctx.enter_context(tc.psum_pool(name="psz", bufs=4))
+        psa = ctx.enter_context(tc.psum_pool(name="psa", bufs=4))
+        ctx.enter_context(tc.manual_schedule())
+
+        o_raw = [keep.tile([P, A, 4, KP], BF16, name=f"o_raw{g}") for g in range(G)]
+        x_raw = {}
+        w_raw = [[keep.tile([P, 4, C], BF16, name=f"w_raw{i}_{g}") for g in range(G)] for i in range(2)]
+
+        def load_omega(g, passes=range(A)):
+            for a in passes:
+                nc.sync.dma_start(
+                    out=o_raw[g][:, a, :, :],
+                    in_=omega[a * KP : (a + 1) * KP, g * KP : (g + 1) * KP].rearrange("(p j) f -> p j f", j=4),
+                )
+
+        def load_x(c):
+            x_raw[c] = stage.tile([P, MT, D], BF16, name="x_raw", tag="x_raw", bufs=2)
+            nc.sync.dma_start(out=x_raw[c][:], in_=x[c * W : (c + 1) * W, :].rearrange("(j p) k -> p j k", p=P))
+
+        def load_w(i, g):
+            src = (w_cos, w_sin)[i][g * KP : (g + 1) * KP, :].rearrange("(b t q) c -> t b q c", t=4, q=8)
+            for t in range(4):
+                nc.sync.dma_start(out=w_raw[i][g][:, t, :], in_=src[t])
+
+        bw_rows = keep.tile([P, P], BF16, name="bw_rows")
+        pa_rows = keep.tile([P, P], BF16, name="pa_rows")
+        of_rows = keep.tile([P, P], BF16, name="of_rows")
+        one = keep.tile([P, 1], F32, name="one")
+        nc.vector.memset(bw_rows[:], 0.0)
+        nc.vector.memset(pa_rows[:], 0.0)
+        nc.vector.memset(one[:], 1.0)
+        nc.vector.memset(of_rows[:], 0.0)
+        nc.scalar.dma_start(out=bw_rows[0:8, :], in_=bandwidth.rearrange("(r p) -> r p", p=P))
+        for i, vec in ((0, phase), (1, amp)):
+            for g in range(G):
+                nc.scalar.dma_start(
+                    out=pa_rows[32 * i + 4 * g : 32 * i + 4 * g + 4, :].rearrange("t (b q) -> t b q", q=8),
+                    in_=vec[g * KP : (g + 1) * KP].rearrange("(b t q) -> t b q", t=4, q=8),
+                )
+        nc.scalar.dma_start(out=of_rows[0:4, :], in_=offset_re.rearrange("(r p) -> r p", p=P))
+        nc.scalar.dma_start(out=of_rows[4:8, :], in_=offset_im.rearrange("(r p) -> r p", p=P))
+        scratch = keep.tile([P, 1], F32, name="scratch")
+        nc.scalar.activation(out=scratch[:], in_=one[:], func=AF.Sin)
+        halfpi = keep.tile([P, 1], F32, name="halfpi")
+        nc.vector.tensor_scalar(out=halfpi[:], in0=one[:], scalar1=math.pi / 2, scalar2=None, op0=ALU.mult)
+
+        load_omega(0, [0])
+        load_x(0)
+        load_omega(0, [1])
+        load_x(1)
+        load_omega(1)
+        load_omega(2)
+        load_w(0, 0)
+        load_w(1, 0)
+
+        def late_loads():
+            load_x(2)
+            load_x(3)
+            for g in (1, 2):
+                load_w(0, g)
+                load_w(1, g)
+
+        id_bf = keep.tile([P, P], BF16, name="id_bf")
+        id_f = keep.tile([P, P], F32, name="id_f")
+        make_identity(nc, id_bf[:])
+        make_identity(nc, id_f[:])
+
+        o_codes = [keep.tile([P, A, KP], U32, name=f"o_codes{g}", align_bytes=64) for g in range(G)]
+        o_scales = [keep.tile([P, A, KP], U8, name=f"o_scales{g}", align_bytes=64) for g in range(G)]
+        x_codes = [keep.tile([P, A, W], U32, name=f"x_codes{c}", align_bytes=64) for c in range(NC)]
+        x_scales = [keep.tile([P, A, W], U8, name=f"x_scales{c}", align_bytes=64) for c in range(NC)]
+        w_codes = [[keep.tile([P, C], U32, name=f"w_codes{i}_{g}", align_bytes=64) for g in range(G)] for i in range(3)]
+        w_scales = [[keep.tile([P, C], U8, name=f"w_scales{i}_{g}", align_bytes=64) for g in range(G)] for i in range(3)]
+
+        def mxq(codes, scales, grouped, fmt):
+            nc.vector.quantize_mx(out=codes.bitcast(fmt), scales=scales, in_=grouped)
+
+        o_grp = {}
+
+        def o_lay(g, a, engine, part=(0, 4)):
+            if part[0] == 0:
+                o_grp[g, a] = stage.tile([P, 4 * KP], BF16, name="o_grp", tag="o_grp", bufs=4, align_bytes=64)
+            t_ = o_grp[g, a]
+            dst = t_[:].rearrange("p (t b q j) -> p t b q j", t=4, q=8, j=4)
+            src = o_raw[g][:, a, :, :].rearrange("p j (b t q) -> p t b q j", t=4, q=8)
+            if engine == "v":
+                nc.vector.tensor_copy(out=dst[:, part[0] : part[1]], in_=src[:, part[0] : part[1]])
+            else:
+                for t in range(*part):
+                    nc.scalar.copy(out=dst[:, t], in_=src[:, t])
+
+        def o_quant(g, a, part=(0, 4)):
+            cols = slice(P * part[0], P * part[1])
+            mxq(o_codes[g][:, a, cols], o_scales[g][:, a, cols], o_grp[g, a][:, 4 * P * part[0] : 4 * P * part[1]], E4)
+
+        w_grp = {}
+
+        def w_lay(i, g, engine):
+            t_ = stage.tile([P, 4 * C], BF16, name="w_grp", tag="w_grp", bufs=2, align_bytes=64)
+            w_grp[i, g] = t_
+            dst = t_[:].rearrange("p (c i t) -> p c t i", i=4, t=4)
+            src = w_raw[i][g][:].rearrange("p t (c i) -> p c t i", i=4)
+            if engine == "v":
+                nc.vector.tensor_copy(out=dst, in_=src)
+            else:
+                nc.scalar.copy(out=dst, in_=src)
+
+        def w_quant(i, g):
+            t_ = w_grp.pop((i, g))
+            if i == 1:
+                n_ = stage.tile([P, 4 * C], BF16, name="w_neg", tag="w_neg", bufs=1, align_bytes=64)
+                nc.vector.tensor_scalar(out=n_[:], in0=t_[:], scalar1=-1.0, scalar2=None, op0=ALU.mult)
+            mxq(w_codes[i][g][:], w_scales[i][g][:], t_[:], E4)
+            if i == 1:
+                mxq(w_codes[2][g][:], w_scales[2][g][:], n_[:], E4)
+
+        x_grp = {}
+
+        def x_turn(c):
+            xg = stage.tile([P, A, W * 4], BF16, name="x_grp", tag="x_grp", bufs=2, align_bytes=64)
+            x_grp[c] = xg
+            for j in range(MT):
+                words = x_raw[c][:, j, :].bitcast(F32)
+                tp = psz.tile([P, 4, P], F32, name="tp", tag="z")
+                for a in range(A):
+                    for u in range(2):
+                        nc.tensor.transpose(tp[:, 2 * a + u, :], words[:, 256 * a + u : 256 * (a + 1) : 2], id_f[:])
+                nc.scalar.copy(
+                    out=xg[:, :, 4 * P * j : 4 * P * (j + 1)].bitcast(F32).rearrange("p a (r u) -> p a r u", u=2),
+                    in_=tp[:].rearrange("p (a u) r -> p a r u", u=2),
+                )
+
+        def x_quant(c):
+            for a in range(A):
+                mxq(x_codes[c][:, a, :], x_scales[c][:, a, :], x_grp[c][:, a, :], E4)
+
+        def turn_rows(rows, name):
+            tp = psa.tile([P, P], BF16, name="rows_t", tag="acc")
+            nc.tensor.transpose(tp[:], rows[:], id_bf[:])
+            ct = keep.tile([P, P], BF16, name=name)
+            nc.scalar.copy(out=ct[:], in_=tp[:])
+            return ct
+
+        def spread(ct):
+            tp = psa.tile([P, 8 * P], BF16, name="spread", tag="acc")
+            for r in range(8):
+                nc.tensor.transpose(tp[:, P * r : P * (r + 1)], ct[:, r : r + 1].to_broadcast([P, P]), id_bf[:])
+            return tp
+
+        bwp = spread(turn_rows(bw_rows, "bw_t"))
+        bwt = keep.tile([P, M], F32, name="bwt")
+        nc.scalar.activation(out=bwt[:], in_=bwp[:], func=AF.Copy, scale=1.0 / TWO_PI)
+        pa_t = turn_rows(pa_rows, "pa_t")
+        x_turn(0)
+        of_t = turn_rows(of_rows, "of_t")
+        phi = keep.tile([P, 4 * G], F32, name="phi")
+        off = keep.tile([P, 2 * C], BF16, name="off")
+
+        units = [(0, 0), (1, 0), (0, 1), (1, 1), (0, 2), (1, 2)] + [(c, g) for c in (2, 3) for g in range(G)]
+        NU = len(units)
+        zt, ut, kt, ft, sin_t, cos_t, gs_t, gc_t = {}, {}, {}, {}, {}, {}, {}, {}
+        f_codes, f_scales = {}, {}
+
+        def stage1(n, banks=range(4 // TPB)):
+            c, g = units[n]
+            if banks[0] == 0:
+                zt[n] = []
+            for b in banks:
+                z = psz.tile([P, TPB, W], F32, name="z", tag="z")
+                zt[n].append(z)
+                for i in range(TPB):
+                    cols = slice(P * (TPB * b + i), P * (TPB * b + i + 1))
+                    for a in range(A):
+                        nc.tensor.matmul_mx(
+                            out=z[:, i, :],
+                            lhsT=o_codes[g][:, a, cols].bitcast(E4),
+                            lhsT_scale=o_scales[g][:, a, cols],
+                            rhs=x_codes[c][:, a, :].bitcast(E4),
+                            rhs_scale=x_scales[c][:, a, :],
+                            start=(a == 0),
+                            stop=(a == A - 1),
+                        )
+
+        def turns(n, banks=range(4 // TPB)):
+            c, g = units[n]
+            if banks[0] == 0:
+                ut[n] = work.tile([P, 4, W], F32, name="u", tag="u", bufs=3)
+            u = ut[n]
+            bw = bwt[:, W * c : W * (c + 1)].unsqueeze(1).to_broadcast([P, TPB, W])
+            for b in banks:
+                nc.vector.tensor_tensor(out=u[:, TPB * b : TPB * (b + 1), :], in0=zt[n][b][:], in1=bw, op=ALU.mult)
+
+        def nearest(n):
+            c, g = units[n]
+            k = work.tile([P, 4, W], I32, name="k", tag="k", bufs=1)
+            kt[n] = k
+            for t in range(4):
+                ph = phi[:, 4 * g + t : 4 * g + t + 1]
+                if t < N_GP:
+                    nc.gpsimd.tensor_scalar(out=k[:, t, :], in0=ut[n][:, t, :], scalar1=1.0, scalar2=ph, op0=ALU.mult, op1=ALU.add)
+                else:
+                    nc.vector.tensor_scalar(out=k[:, t, :], in0=ut[n][:, t, :], scalar1=ph, scalar2=None, op0=ALU.add)
+
+        def reduce(n):
+            c, g = units[n]
+            f = work.tile([P, 4, W], F32, name="f", tag="f", bufs=2)
+            ft[n] = f
+            u, k = ut.pop(n), kt.pop(n)
+            for t in range(4):
+                nc.vector.scalar_tensor_tensor(
+                    out=f[:, t, :], in0=u[:, t, :], scalar=phi[:, 4 * g + t : 4 * g + t + 1], in1=k[:, t, :], op0=ALU.add, op1=ALU.subtract
+                )
+
+        def trig(n):
+            f = ft.pop(n)
+            s = work.tile([P, 4, W], F32, name="s", tag="s", bufs=2)
+            d = work.tile([P, 4, W], F32, name="d", tag="d", bufs=1)
+            co = work.tile([P, 4, W], F32, name="co", tag="co", bufs=2)
+            nc.scalar.activation(out=s[:], in_=f[:], func=AF.Sin, scale=TWO_PI)
+            nc.scalar.activation(out=d[:], in_=f[:], func=AF.Abs)
+            nc.scalar.activation(out=co[:], in_=d[:], func=AF.Sin, scale=-TWO_PI, bias=halfpi[:])
+            sin_t[n], cos_t[n] = s, co
+
+        def scale_amp(n, src, name):
+            c, g = units[n]
+            grp = work.tile([P, 4 * W], BF16, name=name, tag=name, bufs=3, align_bytes=64)
+            am = pa_t[:, 32 + 4 * g : 36 + 4 * g].unsqueeze(1).unsqueeze(3).to_broadcast([P, W // 2, 4, 2])
+            nc.vector.tensor_tensor(
+                out=grp[:].rearrange("p (c i t) -> p c t i", i=2, t=4),
+                in0=src[:].rearrange("p t (c i) -> p c t i", i=2),
+                in1=am,
+                op=ALU.mult,
+            )
+            return grp
+
+        def feat_quant(n):
+            for i, grp in enumerate((gc_t.pop(n), gs_t.pop(n))):
+                co = work.tile([P, W], U32, name=f"f_codes{i}", tag=f"f_codes{i}", bufs=8, align_bytes=64)
+                sc = work.tile([P, W], U8, name=f"f_scales{i}", tag=f"f_scales{i}", bufs=8, align_bytes=64)
+                f_codes[units[n], i], f_scales[units[n], i] = co, sc
+                mxq(co[:], sc[:], grp[:], E5)
+
+        acc = {}
+
+        def stage2(c, mt, gs):
+            rows = slice(P * mt, P * (mt + 1))
+            if (c, mt) not in acc:
+                re_ = psa.tile([P, C], F32, name="re", tag="acc")
+                im_ = psa.tile([P, C], F32, name="im", tag="acc")
+                acc[c, mt] = (re_, im_)
+            re_, im_ = acc[c, mt]
+            for g in gs:
+                for i, pair in ((0, ((re_, 0), (im_, 2))), (1, ((re_, 1), (im_, 0)))):
+                    for o, w in pair:
+                        nc.tensor.matmul_mx(
+                            out=o[:],
+                            lhsT=f_codes[(c, g), i][:, rows].bitcast(E5),
+                            lhsT_scale=f_scales[(c, g), i][:, rows],
+                            rhs=w_codes[w][g][:].bitcast(E4),
+                            rhs_scale=w_scales[w][g][:],
+                            start=(g == 0 and i == 0),
+                            stop=(g == G - 1 and i == 1),
+                        )
+
+        def finish(c, mt):
+            for i, (o, dst) in enumerate(zip(acc.pop((c, mt)), (out_re, out_im))):
+                r = work.tile([P, C], F32, name="r", tag="r", bufs=4)
+                nc.vector.tensor_tensor(out=r[:], in0=o[:], in1=off[:, C * i : C * (i + 1)], op=ALU.add)
+                nc.sync.dma_start(out=dst[c * W + P * mt : c * W + P * (mt + 1), :], in_=r[:])
+
+        o_lay(0, 0, "v")
+        nc.vector.tensor_scalar(out=phi[:], in0=pa_t[:, 0 : 4 * G], scalar1=1.0 / TWO_PI, scalar2=None, op0=ALU.mult)
+        o_quant(0, 0)
+        o_lay(0, 1, "v", (0, 2))
+        x_quant(0)
+        o_quant(0, 1, (0, 2))
+        o_lay(0, 1, "v", (2, 4))
+        stage1(0, [0])
+        x_turn(1)
+        ofp = spread(of_t)
+        nc.scalar.copy(out=off[:], in_=ofp[:])
+        late_loads()
+        turns(0, [0])
+        o_quant(0, 1, (2, 4))
+        stage1(0, [1])
+
+        dve_lay = {0: [("o", 1, 0)]}
+        act_lay = {0: [("o", 1, 1), ("o", 2, 0), ("o", 2, 1)], 1: [(0, 0)], 2: [(1, 0)], 3: [(0, 1)], 4: [(1, 1)], 5: [(0, 2)], 6: [(1, 2)]}
+        early = {0: [("x", 1)]}
+        late = {
+            1: [("o", 1, 0), ("o", 1, 1)], 2: [("o", 2, 0), ("o", 2, 1)], 3: [("w", 0, 0)], 4: [("w", 1, 0), ("x", 2)], 5: [("w", 0, 1)], 6: [("w", 1, 1)],
+            7: [("w", 0, 2), ("x", 3)], 8: [("w", 1, 2)],
+        }
+        turn = {3: 2, 6: 3}
+        mm2 = {
+            8: [(0, 0, (0, 1, 2)), (0, 1, (0, 1, 2))], 9: [(1, 0, (0, 1, 2))], 10: [(1, 1, (0, 1, 2))],
+            11: [(2, 0, (0, 1, 2)), (2, 1, (0, 1, 2))], 12: [(3, 0, (0,)), (3, 1, (0,))], 13: [(3, 0, (1,)), (3, 1, (1,)), (3, 0, (2,)), (3, 1, (2,))],
+        }
+        fin = {9: [(0, 0)], 10: [(1, 0)], 11: [(1, 1)], 12: [(2, 0)], 14: [(3, 0), (3, 1)]}
+        fin2 = {9: [(0, 1)], 12: [(2, 1)]}
+
+        def do_quants(tasks):
+            for task in tasks:
+                if task[0] == "x":
+                    x_quant(task[1])
+                elif task[0] == "o":
+                    o_quant(task[1], task[2])
+                else:
+                    w_quant(task[1], task[2])
+
+        def lay(tasks, engine):
+            for task in tasks:
+                if task[0] == "o":
+                    o_lay(task[1], task[2], engine)
+                else:
+                    w_lay(task[0], task[1], engine)
+
+        for n in range(NU + 3):
+            last = n >= NU
+            if n == 0:
+                turns(0, [1])
+            elif n < NU:
+                turns(n)
+            if 0 <= n - 1 < NU:
+                nearest(n - 1)
+            if n == NU:
+                reduce(n - 1)
+                trig(n - 1)
+            do_quants(early.get(n, []))
+            if n in turn:
+                x_turn(turn[n])
+            lay(dve_lay.get(n, []), "v")
+            if 0 <= n - 3 and n <= NU:
+                feat_quant(n - 3)
+            do_quants(late.get(n, []))
+            if n + 1 < NU:
+                stage1(n + 1)
+            if 0 <= n - 2 < NU:
+                gs_t[n - 2] = scale_amp(n - 2, sin_t.pop(n - 2), "gs")
+            for c, mt in fin.get(n, []):
+                finish(c, mt)
+            if 0 <= n - 2 < NU:
+                gc_t[n - 2] = scale_amp(n - 2, cos_t.pop(n - 2), "gc")
+            for c, mt in fin2.get(n, []):
+                finish(c, mt)
+            if 0 <= n - 1 < NU and not last:
+                reduce(n - 1)
+                trig(n - 1)
+            lay(act_lay.get(n, []), "s")
+            if last and n - 2 < NU:
+                feat_quant(n - 2)
+            for c, mt, gs in mm2.get(n, []):
+                stage2(c, mt, gs)

@@ -21,12 +21,15 @@ P = 128
 KP = 512
 A = D // KP
 G = F // KP
-W = 256
-NC = M // W
-MT = W // P
-TPB = 512 // W
+PW = 256
+CHUNKS = [(0, 256), (256, 256), (512, 256), (768, 256)]
+UNITS = [(0, 0), (1, 0), (0, 1), (1, 1), (0, 2), (1, 2), (2, 0), (2, 1), (2, 2), (3, 0), (3, 1), (3, 2)]
+B_U, B_K, B_F, B_S, B_D, B_CO, B_SB = 3, 1, 2, 1, 1, 2, 2
+NU = len(UNITS)
 TWO_PI = 2.0 * math.pi
-N_GP = 3
+N_GP = 2
+N_GRP = 2
+AMP_ACT = (tuple(range(12)), (3, 5, 7, 8, 9, 10))
 
 
 def tile_complex_fourier_regression_f3_kernel(
@@ -39,27 +42,25 @@ def tile_complex_fourier_regression_f3_kernel(
         work = ctx.enter_context(tc.tile_pool(name="work", bufs=2))
         psz = ctx.enter_context(tc.psum_pool(name="psz", bufs=4))
         psa = ctx.enter_context(tc.psum_pool(name="psa", bufs=4))
-        ctx.enter_context(tc.manual_schedule())
 
-        o_raw = [keep.tile([P, A, 4, KP], BF16, name=f"o_raw{g}") for g in range(G)]
-        x_raw = {}
-        w_raw = [[keep.tile([P, 4, C], BF16, name=f"w_raw{i}_{g}") for g in range(G)] for i in range(2)]
+        o_raw, w_raw, x_raw = {}, {}, {}
 
-        def load_omega(g, passes=range(A)):
-            for a in passes:
-                nc.sync.dma_start(
-                    out=o_raw[g][:, a, :, :],
-                    in_=omega[a * KP : (a + 1) * KP, g * KP : (g + 1) * KP].rearrange("(p j) f -> p j f", j=4),
-                )
+        def load_omega(g, a):
+            o_raw[g, a] = stage.tile([P, 4, KP], BF16, name="raw", tag="raw", bufs=7)
+            nc.sync.dma_start(
+                out=o_raw[g, a][:],
+                in_=omega[a * KP : (a + 1) * KP, g * KP : (g + 1) * KP].rearrange("(p j) f -> p j f", j=4),
+            )
 
-        def load_x(c):
-            x_raw[c] = stage.tile([P, MT, D], BF16, name="x_raw", tag="x_raw", bufs=2)
-            nc.sync.dma_start(out=x_raw[c][:], in_=x[c * W : (c + 1) * W, :].rearrange("(j p) k -> p j k", p=P))
+        def load_x(p):
+            x_raw[p] = stage.tile([P, 2, D], BF16, name="x_raw", tag="x_raw", bufs=2)
+            nc.sync.dma_start(out=x_raw[p][:], in_=x[p * PW : (p + 1) * PW, :].rearrange("(j p) k -> p j k", p=P))
 
         def load_w(i, g):
+            w_raw[i, g] = stage.tile([P, 4, C], BF16, name="raw", tag="raw", bufs=7)
             src = (w_cos, w_sin)[i][g * KP : (g + 1) * KP, :].rearrange("(b t q) c -> t b q c", t=4, q=8)
             for t in range(4):
-                nc.sync.dma_start(out=w_raw[i][g][:, t, :], in_=src[t])
+                nc.sync.dma_start(out=w_raw[i, g][:, t, :], in_=src[t])
 
         bw_rows = keep.tile([P, P], BF16, name="bw_rows")
         pa_rows = keep.tile([P, P], BF16, name="pa_rows")
@@ -83,21 +84,21 @@ def tile_complex_fourier_regression_f3_kernel(
         halfpi = keep.tile([P, 1], F32, name="halfpi")
         nc.vector.tensor_scalar(out=halfpi[:], in0=one[:], scalar1=math.pi / 2, scalar2=None, op0=ALU.mult)
 
-        load_omega(0, [0])
+        load_omega(0, 0)
         load_x(0)
-        load_omega(0, [1])
+        load_omega(0, 1)
         load_x(1)
-        load_omega(1)
-        load_omega(2)
-        load_w(0, 0)
-        load_w(1, 0)
+        load_omega(1, 0)
+        load_omega(1, 1)
 
-        def late_loads():
-            load_x(2)
-            load_x(3)
-            for g in (1, 2):
-                load_w(0, g)
-                load_w(1, g)
+        load_omega(2, 0)
+        load_omega(2, 1)
+        load_w(0, 0)
+        late_load = {
+            0: [(load_w, (1, 0)), (load_w, (0, 1))],
+            1: [(load_x, (2,)), (load_w, (1, 1)), (load_w, (0, 2))],
+            2: [(load_w, (1, 2)), (load_x, (3,))],
+        }
 
         id_bf = keep.tile([P, P], BF16, name="id_bf")
         id_f = keep.tile([P, P], F32, name="id_f")
@@ -106,10 +107,20 @@ def tile_complex_fourier_regression_f3_kernel(
 
         o_codes = [keep.tile([P, A, KP], U32, name=f"o_codes{g}", align_bytes=64) for g in range(G)]
         o_scales = [keep.tile([P, A, KP], U8, name=f"o_scales{g}", align_bytes=64) for g in range(G)]
-        x_codes = [keep.tile([P, A, W], U32, name=f"x_codes{c}", align_bytes=64) for c in range(NC)]
-        x_scales = [keep.tile([P, A, W], U8, name=f"x_scales{c}", align_bytes=64) for c in range(NC)]
-        w_codes = [[keep.tile([P, C], U32, name=f"w_codes{i}_{g}", align_bytes=64) for g in range(G)] for i in range(3)]
-        w_scales = [[keep.tile([P, C], U8, name=f"w_scales{i}_{g}", align_bytes=64) for g in range(G)] for i in range(3)]
+        x_codes = [keep.tile([P, A, w], U32, name=f"x_codes{c}", align_bytes=64) for c, (m0, w) in enumerate(CHUNKS)]
+        x_scales = [keep.tile([P, A, w], U8, name=f"x_scales{c}", align_bytes=64) for c, (m0, w) in enumerate(CHUNKS)]
+        w_shape = ([P, C], [P, 2, C])
+        w_codes = [[keep.tile(w_shape[i], U32, name=f"w_codes{i}_{g}", align_bytes=64) for g in range(G)] for i in range(2)]
+        w_scales = [[keep.tile(w_shape[i], U8, name=f"w_scales{i}_{g}", align_bytes=64) for g in range(G)] for i in range(2)]
+
+        def w_side(tiles, w, g):
+            return tiles[0][g][:] if w == 0 else tiles[1][g][:, w - 1, :]
+        f_codes = {
+            (c, g): keep.tile([P, 2, w], U32, name=f"f_codes{c}_{g}", align_bytes=64) for c, (m0, w) in enumerate(CHUNKS) for g in range(G)
+        }
+        f_scales = {
+            (c, g): keep.tile([P, 2, w], U8, name=f"f_scales{c}_{g}", align_bytes=64) for c, (m0, w) in enumerate(CHUNKS) for g in range(G)
+        }
 
         def mxq(codes, scales, grouped, fmt):
             nc.vector.quantize_mx(out=codes.bitcast(fmt), scales=scales, in_=grouped)
@@ -118,10 +129,9 @@ def tile_complex_fourier_regression_f3_kernel(
 
         def o_lay(g, a, engine, part=(0, 4)):
             if part[0] == 0:
-                o_grp[g, a] = stage.tile([P, 4 * KP], BF16, name="o_grp", tag="o_grp", bufs=4, align_bytes=64)
-            t_ = o_grp[g, a]
-            dst = t_[:].rearrange("p (t b q j) -> p t b q j", t=4, q=8, j=4)
-            src = o_raw[g][:, a, :, :].rearrange("p j (b t q) -> p t b q j", t=4, q=8)
+                o_grp[g, a] = stage.tile([P, 4 * KP], BF16, name="o_grp", tag="o_grp", bufs=3, align_bytes=64)
+            dst = o_grp[g, a][:].rearrange("p (t b q j) -> p t b q j", t=4, q=8, j=4)
+            src = o_raw[g, a][:].rearrange("p j (b t q) -> p t b q j", t=4, q=8)
             if engine == "v":
                 nc.vector.tensor_copy(out=dst[:, part[0] : part[1]], in_=src[:, part[0] : part[1]])
             else:
@@ -135,10 +145,10 @@ def tile_complex_fourier_regression_f3_kernel(
         w_grp = {}
 
         def w_lay(i, g, engine):
-            t_ = stage.tile([P, 4 * C], BF16, name="w_grp", tag="w_grp", bufs=2, align_bytes=64)
+            t_ = stage.tile([P, 1 + i, 4 * C], BF16, name=f"w_grp{i}", tag=f"w_grp{i}", bufs=1, align_bytes=64)
             w_grp[i, g] = t_
-            dst = t_[:].rearrange("p (c i t) -> p c t i", i=4, t=4)
-            src = w_raw[i][g][:].rearrange("p t (c i) -> p c t i", i=4)
+            dst = t_[:, 0, :].rearrange("p (c i t) -> p c t i", i=4, t=4)
+            src = w_raw[i, g][:].rearrange("p t (c i) -> p c t i", i=4)
             if engine == "v":
                 nc.vector.tensor_copy(out=dst, in_=src)
             else:
@@ -146,20 +156,25 @@ def tile_complex_fourier_regression_f3_kernel(
 
         def w_quant(i, g):
             t_ = w_grp.pop((i, g))
-            if i == 1:
-                n_ = stage.tile([P, 4 * C], BF16, name="w_neg", tag="w_neg", bufs=1, align_bytes=64)
-                nc.vector.tensor_scalar(out=n_[:], in0=t_[:], scalar1=-1.0, scalar2=None, op0=ALU.mult)
-            mxq(w_codes[i][g][:], w_scales[i][g][:], t_[:], E4)
-            if i == 1:
-                mxq(w_codes[2][g][:], w_scales[2][g][:], n_[:], E4)
+            if i == 0:
+                mxq(w_codes[0][g][:], w_scales[0][g][:], t_[:, 0, :], E4)
+            else:
+                nc.vector.tensor_scalar(out=t_[:, 1, :], in0=t_[:, 0, :], scalar1=-1.0, scalar2=None, op0=ALU.mult)
+                mxq(
+                    w_codes[1][g][:].rearrange("p i c -> p (i c)"),
+                    w_scales[1][g][:].rearrange("p i c -> p (i c)"),
+                    t_[:].rearrange("p i c -> p (i c)"),
+                    E4,
+                )
 
         x_grp = {}
+        X_HOME = {0: (0, 0), 1: (1, 0), 2: (2, 0), 3: (3, 0)}
 
-        def x_turn(c):
-            xg = stage.tile([P, A, W * 4], BF16, name="x_grp", tag="x_grp", bufs=2, align_bytes=64)
-            x_grp[c] = xg
-            for j in range(MT):
-                words = x_raw[c][:, j, :].bitcast(F32)
+        def x_turn(p):
+            xg = stage.tile([P, A, PW * 4], BF16, name="x_grp", tag="x_grp", bufs=2, align_bytes=64)
+            x_grp[p] = xg
+            for j in range(2):
+                words = x_raw[p][:, j, :].bitcast(F32)
                 tp = psz.tile([P, 4, P], F32, name="tp", tag="z")
                 for a in range(A):
                     for u in range(2):
@@ -169,9 +184,10 @@ def tile_complex_fourier_regression_f3_kernel(
                     in_=tp[:].rearrange("p (a u) r -> p a r u", u=2),
                 )
 
-        def x_quant(c):
+        def x_quant(p):
+            c, m0 = X_HOME[p]
             for a in range(A):
-                mxq(x_codes[c][:, a, :], x_scales[c][:, a, :], x_grp[c][:, a, :], E4)
+                mxq(x_codes[c][:, a, m0 : m0 + PW], x_scales[c][:, a, m0 : m0 + PW], x_grp[p][:, a, :], E4)
 
         def turn_rows(rows, name):
             tp = psa.tile([P, P], BF16, name="rows_t", tag="acc")
@@ -193,22 +209,26 @@ def tile_complex_fourier_regression_f3_kernel(
         x_turn(0)
         of_t = turn_rows(of_rows, "of_t")
         phi = keep.tile([P, 4 * G], F32, name="phi")
+        ampf = keep.tile([P, 4 * G], F32, name="ampf")
         off = keep.tile([P, 2 * C], BF16, name="off")
 
-        units = [(0, 0), (1, 0), (0, 1), (1, 1), (0, 2), (1, 2)] + [(c, g) for c in (2, 3) for g in range(G)]
-        NU = len(units)
-        zt, ut, kt, ft, sin_t, cos_t, gs_t, gc_t = {}, {}, {}, {}, {}, {}, {}, {}
-        f_codes, f_scales = {}, {}
+        zt, ut, kt, ft, trig_t, grp_t = {}, {}, {}, {}, {}, {}
 
-        def stage1(n, banks=range(4 // TPB)):
-            c, g = units[n]
+        def width(n):
+            return CHUNKS[UNITS[n][0]][1]
+
+        def stage1(n, banks=None):
+            c, g = UNITS[n]
+            w = width(n)
+            tpb = 512 // w
+            banks = banks or range(4 // tpb)
             if banks[0] == 0:
                 zt[n] = []
             for b in banks:
-                z = psz.tile([P, TPB, W], F32, name="z", tag="z")
+                z = psz.tile([P, tpb, w], F32, name="z", tag="z")
                 zt[n].append(z)
-                for i in range(TPB):
-                    cols = slice(P * (TPB * b + i), P * (TPB * b + i + 1))
+                for i in range(tpb):
+                    cols = slice(P * (tpb * b + i), P * (tpb * b + i + 1))
                     for a in range(A):
                         nc.tensor.matmul_mx(
                             out=z[:, i, :],
@@ -220,29 +240,32 @@ def tile_complex_fourier_regression_f3_kernel(
                             stop=(a == A - 1),
                         )
 
-        def turns(n, banks=range(4 // TPB)):
-            c, g = units[n]
+        def turns(n, banks=None):
+            c, g = UNITS[n]
+            m0, w = CHUNKS[c]
+            tpb = 512 // w
+            banks = banks or range(4 // tpb)
             if banks[0] == 0:
-                ut[n] = work.tile([P, 4, W], F32, name="u", tag="u", bufs=3)
-            u = ut[n]
-            bw = bwt[:, W * c : W * (c + 1)].unsqueeze(1).to_broadcast([P, TPB, W])
+                ut[n] = work.tile([P, 4, w], F32, name="u", tag="u", bufs=B_U)
+            bw = bwt[:, m0 : m0 + w].unsqueeze(1).to_broadcast([P, tpb, w])
             for b in banks:
-                nc.vector.tensor_tensor(out=u[:, TPB * b : TPB * (b + 1), :], in0=zt[n][b][:], in1=bw, op=ALU.mult)
+                nc.vector.tensor_tensor(out=ut[n][:, tpb * b : tpb * (b + 1), :], in0=zt[n][b][:], in1=bw, op=ALU.mult)
 
-        def nearest(n):
-            c, g = units[n]
-            k = work.tile([P, 4, W], I32, name="k", tag="k", bufs=1)
-            kt[n] = k
+        def nearest(n, gp, dve):
+            c, g = UNITS[n]
+            if gp:
+                kt[n] = work.tile([P, 4, width(n)], I32, name="k", tag="k", bufs=B_K)
+            k = kt[n]
             for t in range(4):
                 ph = phi[:, 4 * g + t : 4 * g + t + 1]
-                if t < N_GP:
+                if t < N_GP and gp:
                     nc.gpsimd.tensor_scalar(out=k[:, t, :], in0=ut[n][:, t, :], scalar1=1.0, scalar2=ph, op0=ALU.mult, op1=ALU.add)
-                else:
+                if t >= N_GP and dve:
                     nc.vector.tensor_scalar(out=k[:, t, :], in0=ut[n][:, t, :], scalar1=ph, scalar2=None, op0=ALU.add)
 
         def reduce(n):
-            c, g = units[n]
-            f = work.tile([P, 4, W], F32, name="f", tag="f", bufs=2)
+            c, g = UNITS[n]
+            f = work.tile([P, 4, width(n)], F32, name="f", tag="f", bufs=B_F)
             ft[n] = f
             u, k = ut.pop(n), kt.pop(n)
             for t in range(4):
@@ -251,33 +274,49 @@ def tile_complex_fourier_regression_f3_kernel(
                 )
 
         def trig(n):
+            c, g = UNITS[n]
+            w = width(n)
             f = ft.pop(n)
-            s = work.tile([P, 4, W], F32, name="s", tag="s", bufs=2)
-            d = work.tile([P, 4, W], F32, name="d", tag="d", bufs=1)
-            co = work.tile([P, 4, W], F32, name="co", tag="co", bufs=2)
+            s = work.tile([P, 4, w], F32, name="s", tag="s", bufs=B_S)
+            d = work.tile([P, 4, w], F32, name="d", tag="d", bufs=B_D)
+            co = work.tile([P, 4, w], F32, name="co", tag="co", bufs=B_CO)
             nc.scalar.activation(out=s[:], in_=f[:], func=AF.Sin, scale=TWO_PI)
             nc.scalar.activation(out=d[:], in_=f[:], func=AF.Abs)
             nc.scalar.activation(out=co[:], in_=d[:], func=AF.Sin, scale=-TWO_PI, bias=halfpi[:])
-            sin_t[n], cos_t[n] = s, co
+            trig_t[n] = [co, s]
+            for i, name in ((1, "sb"), (0, "cb")):
+                if n in AMP_ACT[1 - i]:
+                    src = trig_t[n][i]
+                    trig_t[n][i] = work.tile([P, 4, w], BF16, name=name, tag=name, bufs=B_SB, align_bytes=64)
+                    for t in range(4):
+                        nc.scalar.activation(out=trig_t[n][i][:, t, :], in_=src[:, t, :], func=AF.Copy, scale=ampf[:, 4 * g + t : 4 * g + t + 1])
 
-        def scale_amp(n, src, name):
-            c, g = units[n]
-            grp = work.tile([P, 4 * W], BF16, name=name, tag=name, bufs=3, align_bytes=64)
-            am = pa_t[:, 32 + 4 * g : 36 + 4 * g].unsqueeze(1).unsqueeze(3).to_broadcast([P, W // 2, 4, 2])
-            nc.vector.tensor_tensor(
-                out=grp[:].rearrange("p (c i t) -> p c t i", i=2, t=4),
-                in0=src[:].rearrange("p t (c i) -> p c t i", i=2),
-                in1=am,
-                op=ALU.mult,
-            )
-            return grp
+        def group(n, i):
+            if n not in grp_t:
+                grp_t[n] = work.tile([P, 2, 4 * width(n)], BF16, name="grp", tag="grp", bufs=N_GRP, align_bytes=64)
+            return grp_t[n][:, i, :]
+
+        def features(n):
+            c, g = UNITS[n]
+            w = width(n)
+            for i in range(2):
+                src = trig_t[n][i]
+                r = 4 if n in AMP_ACT[1 - i] else 2
+                dst = group(n, i).rearrange("p (c i t) -> p c t i", i=r, t=4)
+                src = src[:].rearrange("p t (c i) -> p c t i", i=r)
+                if r == 4:
+                    nc.vector.tensor_copy(out=dst, in_=src)
+                else:
+                    am = pa_t[:, 32 + 4 * g : 36 + 4 * g].unsqueeze(1).unsqueeze(3).to_broadcast([P, w // 2, 4, 2])
+                    nc.vector.tensor_tensor(out=dst, in0=src, in1=am, op=ALU.mult)
 
         def feat_quant(n):
-            for i, grp in enumerate((gc_t.pop(n), gs_t.pop(n))):
-                co = work.tile([P, W], U32, name=f"f_codes{i}", tag=f"f_codes{i}", bufs=8, align_bytes=64)
-                sc = work.tile([P, W], U8, name=f"f_scales{i}", tag=f"f_scales{i}", bufs=8, align_bytes=64)
-                f_codes[units[n], i], f_scales[units[n], i] = co, sc
-                mxq(co[:], sc[:], grp[:], E5)
+            mxq(
+                f_codes[UNITS[n]][:].rearrange("p i w -> p (i w)"),
+                f_scales[UNITS[n]][:].rearrange("p i w -> p (i w)"),
+                grp_t.pop(n)[:].rearrange("p i w -> p (i w)"),
+                E5,
+            )
 
         acc = {}
 
@@ -293,50 +332,51 @@ def tile_complex_fourier_regression_f3_kernel(
                     for o, w in pair:
                         nc.tensor.matmul_mx(
                             out=o[:],
-                            lhsT=f_codes[(c, g), i][:, rows].bitcast(E5),
-                            lhsT_scale=f_scales[(c, g), i][:, rows],
-                            rhs=w_codes[w][g][:].bitcast(E4),
-                            rhs_scale=w_scales[w][g][:],
+                            lhsT=f_codes[c, g][:, i, rows].bitcast(E5),
+                            lhsT_scale=f_scales[c, g][:, i, rows],
+                            rhs=w_side(w_codes, w, g).bitcast(E4),
+                            rhs_scale=w_side(w_scales, w, g),
                             start=(g == 0 and i == 0),
                             stop=(g == G - 1 and i == 1),
                         )
 
         def finish(c, mt):
+            r0 = CHUNKS[c][0] + P * mt
             for i, (o, dst) in enumerate(zip(acc.pop((c, mt)), (out_re, out_im))):
                 r = work.tile([P, C], F32, name="r", tag="r", bufs=4)
                 nc.vector.tensor_tensor(out=r[:], in0=o[:], in1=off[:, C * i : C * (i + 1)], op=ALU.add)
-                nc.sync.dma_start(out=dst[c * W + P * mt : c * W + P * (mt + 1), :], in_=r[:])
+                nc.sync.dma_start(out=dst[r0 : r0 + P, :], in_=r[:])
 
         o_lay(0, 0, "v")
         nc.vector.tensor_scalar(out=phi[:], in0=pa_t[:, 0 : 4 * G], scalar1=1.0 / TWO_PI, scalar2=None, op0=ALU.mult)
+        nc.vector.tensor_copy(out=ampf[:], in_=pa_t[:, 32 : 32 + 4 * G])
         o_quant(0, 0)
         o_lay(0, 1, "v", (0, 2))
         x_quant(0)
         o_quant(0, 1, (0, 2))
         o_lay(0, 1, "v", (2, 4))
         stage1(0, [0])
-        x_turn(1)
-        ofp = spread(of_t)
-        nc.scalar.copy(out=off[:], in_=ofp[:])
-        late_loads()
         turns(0, [0])
         o_quant(0, 1, (2, 4))
         stage1(0, [1])
+        x_turn(1)
+        ofp = spread(of_t)
+        nc.scalar.copy(out=off[:], in_=ofp[:])
 
-        dve_lay = {0: [("o", 1, 0)]}
-        act_lay = {0: [("o", 1, 1), ("o", 2, 0), ("o", 2, 1)], 1: [(0, 0)], 2: [(1, 0)], 3: [(0, 1)], 4: [(1, 1)], 5: [(0, 2)], 6: [(1, 2)]}
+        dve_lay = {0: [("o", 1, 0), ("o", 1, 1)], 1: [("o", 2, 0)]}
+        act_lay = {0: [("o", 2, 1)], 1: [(0, 0)], 2: [(1, 0)], 3: [(0, 1)], 4: [(1, 1)], 5: [(0, 2)], 6: [(1, 2)]}
         early = {0: [("x", 1)]}
         late = {
-            1: [("o", 1, 0), ("o", 1, 1)], 2: [("o", 2, 0), ("o", 2, 1)], 3: [("w", 0, 0)], 4: [("w", 1, 0), ("x", 2)], 5: [("w", 0, 1)], 6: [("w", 1, 1)],
-            7: [("w", 0, 2), ("x", 3)], 8: [("w", 1, 2)],
+            0: [("o", 1, 0), ("o", 1, 1)], 2: [("o", 2, 0), ("o", 2, 1)], 3: [("w", 0, 0)], 4: [("w", 1, 0), ("x", 2)], 5: [("w", 0, 1)], 6: [("w", 1, 1)], 7: [("x", 3), ("w", 0, 2)],
+            8: [("w", 1, 2)],
         }
         turn = {3: 2, 6: 3}
+        ALL = (0, 1, 2)
         mm2 = {
-            8: [(0, 0, (0, 1, 2)), (0, 1, (0, 1, 2))], 9: [(1, 0, (0, 1, 2))], 10: [(1, 1, (0, 1, 2))],
-            11: [(2, 0, (0, 1, 2)), (2, 1, (0, 1, 2))], 12: [(3, 0, (0,)), (3, 1, (0,))], 13: [(3, 0, (1,)), (3, 1, (1,)), (3, 0, (2,)), (3, 1, (2,))],
+            7: [(0, 0, (0,)), (0, 1, (0,))], 8: [(0, 0, (1,)), (0, 1, (1,))], 9: [(0, 0, (2,)), (0, 1, (2,))], 10: [(1, 0, ALL), (1, 1, ALL)],
+            11: [], 12: [(2, 0, ALL), (2, 1, ALL)], 13: [(3, 0, (0,)), (3, 1, (0,)), (3, 0, (1,)), (3, 1, (1,))], 14: [(3, 0, (2,)), (3, 1, (2,))],
         }
-        fin = {9: [(0, 0)], 10: [(1, 0)], 11: [(1, 1)], 12: [(2, 0)], 14: [(3, 0), (3, 1)]}
-        fin2 = {9: [(0, 1)], 12: [(2, 1)]}
+        fin = {10: [(0, 0), (0, 1)], 11: [(1, 0), (1, 1)], 13: [(2, 0), (2, 1)], 15: [(3, 0), (3, 1)]}
 
         def do_quants(tasks):
             for task in tasks:
@@ -354,39 +394,41 @@ def tile_complex_fourier_regression_f3_kernel(
                 else:
                     w_lay(task[0], task[1], engine)
 
-        for n in range(NU + 3):
+        for n in range(NU + 4):
             last = n >= NU
             if n == 0:
                 turns(0, [1])
             elif n < NU:
                 turns(n)
             if 0 <= n - 1 < NU:
-                nearest(n - 1)
+                nearest(n - 1, True, last)
             if n == NU:
                 reduce(n - 1)
                 trig(n - 1)
+            for c, mt in fin.get(n, []):
+                finish(c, mt)
             do_quants(early.get(n, []))
             if n in turn:
                 x_turn(turn[n])
+            if 0 <= n - 4 < NU and n < NU:
+                feat_quant(n - 4)
             lay(dve_lay.get(n, []), "v")
-            if 0 <= n - 3 and n <= NU:
-                feat_quant(n - 3)
             do_quants(late.get(n, []))
             if n + 1 < NU:
                 stage1(n + 1)
-            if 0 <= n - 2 < NU:
-                gs_t[n - 2] = scale_amp(n - 2, sin_t.pop(n - 2), "gs")
-            for c, mt in fin.get(n, []):
-                finish(c, mt)
-            if 0 <= n - 2 < NU:
-                gc_t[n - 2] = scale_amp(n - 2, cos_t.pop(n - 2), "gc")
-            for c, mt in fin2.get(n, []):
-                finish(c, mt)
+            if 0 <= n - 1 < NU and not last:
+                nearest(n - 1, False, True)
+            if 0 <= n - 3 < NU:
+                features(n - 3)
             if 0 <= n - 1 < NU and not last:
                 reduce(n - 1)
                 trig(n - 1)
             lay(act_lay.get(n, []), "s")
-            if last and n - 2 < NU:
-                feat_quant(n - 2)
+            for f, args in late_load.get(n, []):
+                f(*args)
+            if n == NU:
+                feat_quant(n - 4)
+            if last and n - 3 < NU:
+                feat_quant(n - 3)
             for c, mt, gs in mm2.get(n, []):
                 stage2(c, mt, gs)

@@ -22,14 +22,14 @@ KP = 512
 A = D // KP
 G = F // KP
 PW = 256
-CHUNKS = [(0, 256), (256, 256), (512, 256), (768, 256)]
-UNITS = [(0, 0), (1, 0), (0, 1), (1, 1), (0, 2), (1, 2), (2, 0), (2, 1), (2, 2), (3, 0), (3, 1), (3, 2)]
-B_U, B_K, B_F, B_S, B_D, B_CO, B_SB = 3, 1, 2, 1, 1, 2, 2
+CHUNKS = [(0, 256), (256, 512), (768, 256)]
+UNITS = [(0, 0), (1, 0), (1, 1), (1, 2), (0, 1), (0, 2), (2, 0), (2, 1), (2, 2)]
+B_U, B_K, B_S, B_SB, B_CB = 4, 1, 1, 2, 1
 NU = len(UNITS)
 TWO_PI = 2.0 * math.pi
-N_GP = 2
+N_GP = {512: 3, 256: 2}
 N_GRP = 2
-AMP_ACT = (tuple(range(12)), (3, 5, 7, 8, 9, 10))
+AMP_ACT = (tuple(range(9)), (5, 6, 7))
 
 
 def tile_complex_fourier_regression_f3_kernel(
@@ -52,9 +52,12 @@ def tile_complex_fourier_regression_f3_kernel(
                 in_=omega[a * KP : (a + 1) * KP, g * KP : (g + 1) * KP].rearrange("(p j) f -> p j f", j=4),
             )
 
-        def load_x(p):
-            x_raw[p] = stage.tile([P, 2, D], BF16, name="x_raw", tag="x_raw", bufs=2)
-            nc.sync.dma_start(out=x_raw[p][:], in_=x[p * PW : (p + 1) * PW, :].rearrange("(j p) k -> p j k", p=P))
+        def load_x(p, j=None):
+            if not j:
+                x_raw[p] = stage.tile([P, 2, D], BF16, name="x_raw", tag="x_raw", bufs=2)
+            js = range(2) if j is None else range(j, j + 1)
+            rows = x[p * PW + P * js.start : p * PW + P * js.stop, :]
+            nc.sync.dma_start(out=x_raw[p][:, js.start : js.stop, :], in_=rows.rearrange("(j p) k -> p j k", p=P))
 
         def load_w(i, g):
             w_raw[i, g] = stage.tile([P, 4, C], BF16, name="raw", tag="raw", bufs=7)
@@ -84,8 +87,9 @@ def tile_complex_fourier_regression_f3_kernel(
         halfpi = keep.tile([P, 1], F32, name="halfpi")
         nc.vector.tensor_scalar(out=halfpi[:], in0=one[:], scalar1=math.pi / 2, scalar2=None, op0=ALU.mult)
 
+        load_x(0, 0)
         load_omega(0, 0)
-        load_x(0)
+        load_x(0, 1)
         load_omega(0, 1)
         load_x(1)
         load_omega(1, 0)
@@ -96,8 +100,8 @@ def tile_complex_fourier_regression_f3_kernel(
         load_w(0, 0)
         late_load = {
             0: [(load_w, (1, 0)), (load_w, (0, 1))],
-            1: [(load_x, (2,)), (load_w, (1, 1)), (load_w, (0, 2))],
-            2: [(load_w, (1, 2)), (load_x, (3,))],
+            1: [(load_w, (1, 1)), (load_w, (0, 2)), (load_x, (3,))],
+            2: [(load_w, (1, 2))],
         }
 
         id_bf = keep.tile([P, P], BF16, name="id_bf")
@@ -168,7 +172,7 @@ def tile_complex_fourier_regression_f3_kernel(
                 )
 
         x_grp = {}
-        X_HOME = {0: (0, 0), 1: (1, 0), 2: (2, 0), 3: (3, 0)}
+        X_HOME = {0: (0, 0), 1: (1, 0), 2: (1, PW), 3: (2, 0)}
 
         def x_turn(p):
             xg = stage.tile([P, A, PW * 4], BF16, name="x_grp", tag="x_grp", bufs=2, align_bytes=64)
@@ -212,7 +216,7 @@ def tile_complex_fourier_regression_f3_kernel(
         ampf = keep.tile([P, 4 * G], F32, name="ampf")
         off = keep.tile([P, 2 * C], BF16, name="off")
 
-        zt, ut, kt, ft, trig_t, grp_t = {}, {}, {}, {}, {}, {}
+        zt, ut, kt, trig_t, grp_t = {}, {}, {}, {}, {}
 
         def width(n):
             return CHUNKS[UNITS[n][0]][1]
@@ -258,36 +262,32 @@ def tile_complex_fourier_regression_f3_kernel(
             k = kt[n]
             for t in range(4):
                 ph = phi[:, 4 * g + t : 4 * g + t + 1]
-                if t < N_GP and gp:
+                if t < N_GP[width(n)] and gp:
                     nc.gpsimd.tensor_scalar(out=k[:, t, :], in0=ut[n][:, t, :], scalar1=1.0, scalar2=ph, op0=ALU.mult, op1=ALU.add)
-                if t >= N_GP and dve:
+                if t >= N_GP[width(n)] and dve:
                     nc.vector.tensor_scalar(out=k[:, t, :], in0=ut[n][:, t, :], scalar1=ph, scalar2=None, op0=ALU.add)
 
         def reduce(n):
             c, g = UNITS[n]
-            f = work.tile([P, 4, width(n)], F32, name="f", tag="f", bufs=B_F)
-            ft[n] = f
-            u, k = ut.pop(n), kt.pop(n)
+            u, k = ut[n], kt.pop(n)
             for t in range(4):
                 nc.vector.scalar_tensor_tensor(
-                    out=f[:, t, :], in0=u[:, t, :], scalar=phi[:, 4 * g + t : 4 * g + t + 1], in1=k[:, t, :], op0=ALU.add, op1=ALU.subtract
+                    out=u[:, t, :], in0=u[:, t, :], scalar=phi[:, 4 * g + t : 4 * g + t + 1], in1=k[:, t, :], op0=ALU.add, op1=ALU.subtract
                 )
 
         def trig(n):
             c, g = UNITS[n]
             w = width(n)
-            f = ft.pop(n)
+            f = ut.pop(n)
             s = work.tile([P, 4, w], F32, name="s", tag="s", bufs=B_S)
-            d = work.tile([P, 4, w], F32, name="d", tag="d", bufs=B_D)
-            co = work.tile([P, 4, w], F32, name="co", tag="co", bufs=B_CO)
             nc.scalar.activation(out=s[:], in_=f[:], func=AF.Sin, scale=TWO_PI)
-            nc.scalar.activation(out=d[:], in_=f[:], func=AF.Abs)
-            nc.scalar.activation(out=co[:], in_=d[:], func=AF.Sin, scale=-TWO_PI, bias=halfpi[:])
-            trig_t[n] = [co, s]
-            for i, name in ((1, "sb"), (0, "cb")):
+            nc.scalar.activation(out=f[:], in_=f[:], func=AF.Abs)
+            nc.scalar.activation(out=f[:], in_=f[:], func=AF.Sin, scale=-TWO_PI, bias=halfpi[:])
+            trig_t[n] = [f, s]
+            for i, name, bufs in ((1, "sb", B_SB), (0, "cb", B_CB)):
                 if n in AMP_ACT[1 - i]:
                     src = trig_t[n][i]
-                    trig_t[n][i] = work.tile([P, 4, w], BF16, name=name, tag=name, bufs=B_SB, align_bytes=64)
+                    trig_t[n][i] = work.tile([P, 4, w], BF16, name=name, tag=name, bufs=bufs, align_bytes=64)
                     for t in range(4):
                         nc.scalar.activation(out=trig_t[n][i][:, t, :], in_=src[:, t, :], func=AF.Copy, scale=ampf[:, 4 * g + t : 4 * g + t + 1])
 
@@ -347,14 +347,15 @@ def tile_complex_fourier_regression_f3_kernel(
                 nc.vector.tensor_tensor(out=r[:], in0=o[:], in1=off[:, C * i : C * (i + 1)], op=ALU.add)
                 nc.sync.dma_start(out=dst[r0 : r0 + P, :], in_=r[:])
 
-        o_lay(0, 0, "v")
+        o_lay(0, 0, "v", (0, 3))
+        o_lay(0, 0, "s", (3, 4))
         nc.vector.tensor_scalar(out=phi[:], in0=pa_t[:, 0 : 4 * G], scalar1=1.0 / TWO_PI, scalar2=None, op0=ALU.mult)
         nc.vector.tensor_copy(out=ampf[:], in_=pa_t[:, 32 : 32 + 4 * G])
         o_quant(0, 0)
         o_lay(0, 1, "v", (0, 2))
         x_quant(0)
         o_quant(0, 1, (0, 2))
-        o_lay(0, 1, "v", (2, 4))
+        o_lay(0, 1, "s", (2, 4))
         stage1(0, [0])
         turns(0, [0])
         o_quant(0, 1, (2, 4))
@@ -362,21 +363,22 @@ def tile_complex_fourier_regression_f3_kernel(
         x_turn(1)
         ofp = spread(of_t)
         nc.scalar.copy(out=off[:], in_=ofp[:])
+        load_x(2)
+        x_turn(2)
 
         dve_lay = {0: [("o", 1, 0), ("o", 1, 1)], 1: [("o", 2, 0)]}
-        act_lay = {0: [("o", 2, 1)], 1: [(0, 0)], 2: [(1, 0)], 3: [(0, 1)], 4: [(1, 1)], 5: [(0, 2)], 6: [(1, 2)]}
-        early = {0: [("x", 1)]}
+        act_lay = {0: [("o", 2, 1)], 1: [(0, 0), (1, 0)], 2: [(0, 1), (1, 1)], 3: [(0, 2), (1, 2)]}
+        early = {0: [("x", 1), ("x", 2)]}
         late = {
-            0: [("o", 1, 0), ("o", 1, 1)], 2: [("o", 2, 0), ("o", 2, 1)], 3: [("w", 0, 0)], 4: [("w", 1, 0), ("x", 2)], 5: [("w", 0, 1)], 6: [("w", 1, 1)], 7: [("x", 3), ("w", 0, 2)],
-            8: [("w", 1, 2)],
+            0: [("o", 1, 0), ("o", 1, 1)], 1: [("o", 2, 0), ("o", 2, 1)], 2: [("w", 0, 0), ("w", 1, 0)], 3: [("w", 0, 1), ("w", 1, 1)], 4: [("x", 3), ("w", 0, 2), ("w", 1, 2)],
         }
-        turn = {3: 2, 6: 3}
+        turn = {3: 3}
         ALL = (0, 1, 2)
         mm2 = {
-            7: [(0, 0, (0,)), (0, 1, (0,))], 8: [(0, 0, (1,)), (0, 1, (1,))], 9: [(0, 0, (2,)), (0, 1, (2,))], 10: [(1, 0, ALL), (1, 1, ALL)],
-            11: [], 12: [(2, 0, ALL), (2, 1, ALL)], 13: [(3, 0, (0,)), (3, 1, (0,)), (3, 0, (1,)), (3, 1, (1,))], 14: [(3, 0, (2,)), (3, 1, (2,))],
+            6: [(1, 0, ALL)], 7: [(1, 1, ALL), (1, 2, ALL)], 8: [(1, 3, ALL), (0, 0, ALL)], 9: [(0, 1, ALL)],
+            10: [(2, 0, (0,)), (2, 1, (0,)), (2, 0, (1,)), (2, 1, (1,))], 11: [(2, 0, (2,)), (2, 1, (2,))],
         }
-        fin = {10: [(0, 0), (0, 1)], 11: [(1, 0), (1, 1)], 13: [(2, 0), (2, 1)], 15: [(3, 0), (3, 1)]}
+        fin = {7: [(1, 0)], 8: [(1, 1), (1, 2)], 9: [(1, 3), (0, 0)], 10: [(0, 1)], 12: [(2, 0), (2, 1)]}
 
         def do_quants(tasks):
             for task in tasks:
@@ -410,8 +412,6 @@ def tile_complex_fourier_regression_f3_kernel(
             do_quants(early.get(n, []))
             if n in turn:
                 x_turn(turn[n])
-            if 0 <= n - 4 < NU and n < NU:
-                feat_quant(n - 4)
             lay(dve_lay.get(n, []), "v")
             do_quants(late.get(n, []))
             if n + 1 < NU:
@@ -426,9 +426,7 @@ def tile_complex_fourier_regression_f3_kernel(
             lay(act_lay.get(n, []), "s")
             for f, args in late_load.get(n, []):
                 f(*args)
-            if n == NU:
-                feat_quant(n - 4)
-            if last and n - 3 < NU:
+            if 0 <= n - 3 < NU:
                 feat_quant(n - 3)
             for c, mt, gs in mm2.get(n, []):
                 stage2(c, mt, gs)

@@ -27,9 +27,9 @@ UNITS = [(0, 0), (1, 0), (1, 1), (1, 2), (0, 1), (0, 2), (2, 0), (2, 1), (2, 2)]
 B_U, B_K, B_S, B_SB, B_CB = 4, 1, 1, 2, 1
 NU = len(UNITS)
 TWO_PI = 2.0 * math.pi
-N_GP = {512: 3, 256: 2}
+N_GP = {512: 3, 256: 2, 128: 1}
 N_GRP = 2
-AMP_ACT = (tuple(range(9)), (5, 6, 7))
+AMP_ACT = ((0, 1, 2, 3, 4, 5, 6, 7), (4, 6, 7))
 
 
 def tile_complex_fourier_regression_f3_kernel(
@@ -172,7 +172,6 @@ def tile_complex_fourier_regression_f3_kernel(
                 )
 
         x_grp = {}
-        X_HOME = {0: (0, 0), 1: (1, 0), 2: (1, PW), 3: (2, 0)}
 
         def x_turn(p):
             xg = stage.tile([P, A, PW * 4], BF16, name="x_grp", tag="x_grp", bufs=2, align_bytes=64)
@@ -189,9 +188,19 @@ def tile_complex_fourier_regression_f3_kernel(
                 )
 
         def x_quant(p):
-            c, m0 = X_HOME[p]
-            for a in range(A):
-                mxq(x_codes[c][:, a, m0 : m0 + PW], x_scales[c][:, a, m0 : m0 + PW], x_grp[p][:, a, :], E4)
+            spans = {}
+            for j in range(2):
+                r = p * PW + P * j
+                c = [i for i, (m0, w) in enumerate(CHUNKS) if m0 <= r < m0 + w][0]
+                spans.setdefault(c, []).append(j)
+            for c, js in spans.items():
+                r = p * PW + P * js[0] - CHUNKS[c][0]
+                n = P * len(js)
+                for a in range(A):
+                    mxq(
+                        x_codes[c][:, a, r : r + n], x_scales[c][:, a, r : r + n],
+                        x_grp[p][:, a, 4 * P * js[0] : 4 * (P * js[0] + n)], E4,
+                    )
 
         def turn_rows(rows, name):
             tp = psa.tile([P, P], BF16, name="rows_t", tag="acc")
@@ -367,7 +376,7 @@ def tile_complex_fourier_regression_f3_kernel(
         x_turn(2)
 
         dve_lay = {0: [("o", 1, 0), ("o", 1, 1)], 1: [("o", 2, 0)]}
-        act_lay = {0: [("o", 2, 1)], 1: [(0, 0), (1, 0)], 2: [(0, 1), (1, 1)], 3: [(0, 2), (1, 2)]}
+        act_lay = {0: [("o", 2, 1)], 1: [(0, 0), (1, 0)], 2: [(0, 1), (1, 1), (0, 2)], 3: [(1, 2)]}
         early = {0: [("x", 1), ("x", 2)]}
         late = {
             0: [("o", 1, 0), ("o", 1, 1)], 1: [("o", 2, 0), ("o", 2, 1)], 2: [("w", 0, 0), ("w", 1, 0)], 3: [("w", 0, 1), ("w", 1, 1)], 4: [("x", 3), ("w", 0, 2), ("w", 1, 2)],
@@ -402,13 +411,13 @@ def tile_complex_fourier_regression_f3_kernel(
                 turns(0, [1])
             elif n < NU:
                 turns(n)
+            for c, mt in fin.get(n, []):
+                finish(c, mt)
             if 0 <= n - 1 < NU:
                 nearest(n - 1, True, last)
             if n == NU:
                 reduce(n - 1)
                 trig(n - 1)
-            for c, mt in fin.get(n, []):
-                finish(c, mt)
             do_quants(early.get(n, []))
             if n in turn:
                 x_turn(turn[n])

import math
from contextlib import ExitStack

import concourse.mybir as mybir
from concourse.masks import make_identity

M, D, F, C = 1024, 1024, 1536, 512
FLOPS = 2 * M * D * F + 4 * 2 * M * F * C

F32 = mybir.dt.float32
BF16 = mybir.dt.bfloat16
I32 = mybir.dt.int32
U32 = mybir.dt.uint32
U8 = mybir.dt.uint8
E4 = mybir.dt.float8_e4m3fn_x4
E5 = mybir.dt.float8_e5m2_x4
AF = mybir.ActivationFunctionType
ALU = mybir.AluOpType

P = 128
KP = 512
A = D // KP
G = F // KP
PW = 256
CHUNKS = [(0, 256), (256, 512), (768, 256)]
UNITS = [(0, 0), (1, 0), (1, 1), (1, 2), (0, 1), (0, 2), (2, 0), (2, 1), (2, 2)]
B_U, B_K, B_S, B_SB, B_CB = 4, 1, 1, 2, 1
NU = len(UNITS)
TWO_PI = 2.0 * math.pi
N_GP = {512: 3, 256: 2, 128: 1}
N_GRP = 2
AMP_ACT = ((0, 1, 2, 3, 4, 5, 6, 7), (4, 6, 7))


def tile_complex_fourier_regression_f3_kernel(
    tc, x, omega, bandwidth, phase, amp, w_cos, w_sin, offset_re, offset_im, out_re, out_im
):
    nc = tc.nc
    with ExitStack() as ctx:
        keep = ctx.enter_context(tc.tile_pool(name="keep", bufs=1))
        stage = ctx.enter_context(tc.tile_pool(name="stage", bufs=2))
        work = ctx.enter_context(tc.tile_pool(name="work", bufs=2))
        psz = ctx.enter_context(tc.psum_pool(name="psz", bufs=4))
        psa = ctx.enter_context(tc.psum_pool(name="psa", bufs=4))

        o_raw, w_raw, x_raw = {}, {}, {}

        def load_omega(g, a):
            o_raw[g, a] = stage.tile([P, 4, KP], BF16, name="raw", tag="raw", bufs=7)
            nc.sync.dma_start(
                out=o_raw[g, a][:],
                in_=omega[a * KP : (a + 1) * KP, g * KP : (g + 1) * KP].rearrange("(p j) f -> p j f", j=4),
            )

        def load_x(p, j=None):
            if not j:
                x_raw[p] = stage.tile([P, 2, D], BF16, name="x_raw", tag="x_raw", bufs=2)
            js = range(2) if j is None else range(j, j + 1)
            rows = x[p * PW + P * js.start : p * PW + P * js.stop, :]
            nc.sync.dma_start(out=x_raw[p][:, js.start : js.stop, :], in_=rows.rearrange("(j p) k -> p j k", p=P))

        def load_w(i, g):
            w_raw[i, g] = stage.tile([P, 4, C], BF16, name="raw", tag="raw", bufs=7)
            src = (w_cos, w_sin)[i][g * KP : (g + 1) * KP, :].rearrange("(b t q) c -> t b q c", t=4, q=8)
            for t in range(4):
                nc.sync.dma_start(out=w_raw[i, g][:, t, :], in_=src[t])

        bw_rows = keep.tile([P, P], BF16, name="bw_rows")
        pa_rows = keep.tile([P, P], BF16, name="pa_rows")
        of_rows = keep.tile([P, P], BF16, name="of_rows")
        one = keep.tile([P, 1], F32, name="one")
        nc.vector.memset(bw_rows[:], 0.0)
        nc.vector.memset(pa_rows[:], 0.0)
        nc.vector.memset(one[:], 1.0)
        nc.vector.memset(of_rows[:], 0.0)
        nc.scalar.dma_start(out=bw_rows[0:8, :], in_=bandwidth.rearrange("(r p) -> r p", p=P))
        for i, vec in ((0, phase), (1, amp)):
            for g in range(G):
                nc.scalar.dma_start(
                    out=pa_rows[32 * i + 4 * g : 32 * i + 4 * g + 4, :].rearrange("t (b q) -> t b q", q=8),
                    in_=vec[g * KP : (g + 1) * KP].rearrange("(b t q) -> t b q", t=4, q=8),
                )
        nc.scalar.dma_start(out=of_rows[0:4, :], in_=offset_re.rearrange("(r p) -> r p", p=P))
        nc.scalar.dma_start(out=of_rows[4:8, :], in_=offset_im.rearrange("(r p) -> r p", p=P))
        scratch = keep.tile([P, 1], F32, name="scratch")
        nc.scalar.activation(out=scratch[:], in_=one[:], func=AF.Sin)
        halfpi = keep.tile([P, 1], F32, name="halfpi")
        nc.vector.tensor_scalar(out=halfpi[:], in0=one[:], scalar1=math.pi / 2, scalar2=None, op0=ALU.mult)

        load_x(0, 0)
        load_omega(0, 0)
        load_x(0, 1)
        load_omega(0, 1)
        load_x(1)
        load_omega(1, 0)
        load_omega(1, 1)

        load_omega(2, 0)
        load_omega(2, 1)
        load_w(0, 0)
        late_load = {
            0: [(load_w, (1, 0)), (load_w, (0, 1))],
            1: [(load_w, (1, 1)), (load_w, (0, 2)), (load_x, (3,))],
            2: [(load_w, (1, 2))],
        }

        id_bf = keep.tile([P, P], BF16, name="id_bf")
        id_f = keep.tile([P, P], F32, name="id_f")
        make_identity(nc, id_bf[:])
        make_identity(nc, id_f[:])

        o_codes = [keep.tile([P, A, KP], U32, name=f"o_codes{g}", align_bytes=64) for g in range(G)]
        o_scales = [keep.tile([P, A, KP], U8, name=f"o_scales{g}", align_bytes=64) for g in range(G)]
        x_codes = [keep.tile([P, A, w], U32, name=f"x_codes{c}", align_bytes=64) for c, (m0, w) in enumerate(CHUNKS)]
        x_scales = [keep.tile([P, A, w], U8, name=f"x_scales{c}", align_bytes=64) for c, (m0, w) in enumerate(CHUNKS)]
        w_shape = ([P, C], [P, 2, C])
        w_codes = [[keep.tile(w_shape[i], U32, name=f"w_codes{i}_{g}", align_bytes=64) for g in range(G)] for i in range(2)]
        w_scales = [[keep.tile(w_shape[i], U8, name=f"w_scales{i}_{g}", align_bytes=64) for g in range(G)] for i in range(2)]

        def w_side(tiles, w, g):
            return tiles[0][g][:] if w == 0 else tiles[1][g][:, w - 1, :]
        f_codes = {
            (c, g): keep.tile([P, 2, w], U32, name=f"f_codes{c}_{g}", align_bytes=64) for c, (m0, w) in enumerate(CHUNKS) for g in range(G)
        }
        f_scales = {
            (c, g): keep.tile([P, 2, w], U8, name=f"f_scales{c}_{g}", align_bytes=64) for c, (m0, w) in enumerate(CHUNKS) for g in range(G)
        }

        def mxq(codes, scales, grouped, fmt):
            nc.vector.quantize_mx(out=codes.bitcast(fmt), scales=scales, in_=grouped)

        o_grp = {}

        def o_lay(g, a, engine, part=(0, 4)):
            if part[0] == 0:
                o_grp[g, a] = stage.tile([P, 4 * KP], BF16, name="o_grp", tag="o_grp", bufs=3, align_bytes=64)
            dst = o_grp[g, a][:].rearrange("p (t b q j) -> p t b q j", t=4, q=8, j=4)
            src = o_raw[g, a][:].rearrange("p j (b t q) -> p t b q j", t=4, q=8)
            if engine == "v":
                nc.vector.tensor_copy(out=dst[:, part[0] : part[1]], in_=src[:, part[0] : part[1]])
            else:
                for t in range(*part):
                    nc.scalar.copy(out=dst[:, t], in_=src[:, t])

        def o_quant(g, a, part=(0, 4)):
            cols = slice(P * part[0], P * part[1])
            mxq(o_codes[g][:, a, cols], o_scales[g][:, a, cols], o_grp[g, a][:, 4 * P * part[0] : 4 * P * part[1]], E4)

        w_grp = {}

        def w_lay(i, g, engine):
            t_ = stage.tile([P, 1 + i, 4 * C], BF16, name=f"w_grp{i}", tag=f"w_grp{i}", bufs=1, align_bytes=64)
            w_grp[i, g] = t_
            dst = t_[:, 0, :].rearrange("p (c i t) -> p c t i", i=4, t=4)
            src = w_raw[i, g][:].rearrange("p t (c i) -> p c t i", i=4)
            if engine == "v":
                nc.vector.tensor_copy(out=dst, in_=src)
            else:
                nc.scalar.copy(out=dst, in_=src)

        def w_quant(i, g):
            t_ = w_grp.pop((i, g))
            if i == 0:
                mxq(w_codes[0][g][:], w_scales[0][g][:], t_[:, 0, :], E4)
            else:
                nc.vector.tensor_scalar(out=t_[:, 1, :], in0=t_[:, 0, :], scalar1=-1.0, scalar2=None, op0=ALU.mult)
                mxq(
                    w_codes[1][g][:].rearrange("p i c -> p (i c)"),
                    w_scales[1][g][:].rearrange("p i c -> p (i c)"),
                    t_[:].rearrange("p i c -> p (i c)"),
                    E4,
                )

        x_grp = {}

        def x_turn(p):
            xg = stage.tile([P, A, PW * 4], BF16, name="x_grp", tag="x_grp", bufs=2, align_bytes=64)
            x_grp[p] = xg
            for j in range(2):
                words = x_raw[p][:, j, :].bitcast(F32)
                tp = psz.tile([P, 4, P], F32, name="tp", tag="z")
                for a in range(A):
                    for u in range(2):
                        nc.tensor.transpose(tp[:, 2 * a + u, :], words[:, 256 * a + u : 256 * (a + 1) : 2], id_f[:])
                nc.scalar.copy(
                    out=xg[:, :, 4 * P * j : 4 * P * (j + 1)].bitcast(F32).rearrange("p a (r u) -> p a r u", u=2),
                    in_=tp[:].rearrange("p (a u) r -> p a r u", u=2),
                )

        def x_quant(p):
            spans = {}
            for j in range(2):
                r = p * PW + P * j
                c = [i for i, (m0, w) in enumerate(CHUNKS) if m0 <= r < m0 + w][0]
                spans.setdefault(c, []).append(j)
            for c, js in spans.items():
                r = p * PW + P * js[0] - CHUNKS[c][0]
                n = P * len(js)
                for a in range(A):
                    mxq(
                        x_codes[c][:, a, r : r + n], x_scales[c][:, a, r : r + n],
                        x_grp[p][:, a, 4 * P * js[0] : 4 * (P * js[0] + n)], E4,
                    )

        def turn_rows(rows, name):
            tp = psa.tile([P, P], BF16, name="rows_t", tag="acc")
            nc.tensor.transpose(tp[:], rows[:], id_bf[:])
            ct = keep.tile([P, P], BF16, name=name)
            nc.scalar.copy(out=ct[:], in_=tp[:])
            return ct

        def spread(ct):
            tp = psa.tile([P, 8 * P], BF16, name="spread", tag="acc")
            for r in range(8):
                nc.tensor.transpose(tp[:, P * r : P * (r + 1)], ct[:, r : r + 1].to_broadcast([P, P]), id_bf[:])
            return tp

        bwp = spread(turn_rows(bw_rows, "bw_t"))
        bwt = keep.tile([P, M], F32, name="bwt")
        nc.scalar.activation(out=bwt[:], in_=bwp[:], func=AF.Copy, scale=1.0 / TWO_PI)
        pa_t = turn_rows(pa_rows, "pa_t")
        x_turn(0)
        of_t = turn_rows(of_rows, "of_t")
        phi = keep.tile([P, 4 * G], F32, name="phi")
        ampf = keep.tile([P, 4 * G], F32, name="ampf")
        off = keep.tile([P, 2 * C], BF16, name="off")

        zt, ut, kt, trig_t, grp_t = {}, {}, {}, {}, {}

        def width(n):
            return CHUNKS[UNITS[n][0]][1]

        def stage1(n, banks=None):
            c, g = UNITS[n]
            w = width(n)
            tpb = 512 // w
            banks = banks or range(4 // tpb)
            if banks[0] == 0:
                zt[n] = []
            for b in banks:
                z = psz.tile([P, tpb, w], F32, name="z", tag="z")
                zt[n].append(z)
                for i in range(tpb):
                    cols = slice(P * (tpb * b + i), P * (tpb * b + i + 1))
                    for a in range(A):
                        nc.tensor.matmul_mx(
                            out=z[:, i, :],
                            lhsT=o_codes[g][:, a, cols].bitcast(E4),
                            lhsT_scale=o_scales[g][:, a, cols],
                            rhs=x_codes[c][:, a, :].bitcast(E4),
                            rhs_scale=x_scales[c][:, a, :],
                            start=(a == 0),
                            stop=(a == A - 1),
                        )

        def turns(n, banks=None):
            c, g = UNITS[n]
            m0, w = CHUNKS[c]
            tpb = 512 // w
            banks = banks or range(4 // tpb)
            if banks[0] == 0:
                ut[n] = work.tile([P, 4, w], F32, name="u", tag="u", bufs=B_U)
            bw = bwt[:, m0 : m0 + w].unsqueeze(1).to_broadcast([P, tpb, w])
            for b in banks:
                nc.vector.tensor_tensor(out=ut[n][:, tpb * b : tpb * (b + 1), :], in0=zt[n][b][:], in1=bw, op=ALU.mult)

        def nearest(n, gp, dve):
            c, g = UNITS[n]
            if gp:
                kt[n] = work.tile([P, 4, width(n)], I32, name="k", tag="k", bufs=B_K)
            k = kt[n]
            for t in range(4):
                ph = phi[:, 4 * g + t : 4 * g + t + 1]
                if t < N_GP[width(n)] and gp:
                    nc.gpsimd.tensor_scalar(out=k[:, t, :], in0=ut[n][:, t, :], scalar1=1.0, scalar2=ph, op0=ALU.mult, op1=ALU.add)
                if t >= N_GP[width(n)] and dve:
                    nc.vector.tensor_scalar(out=k[:, t, :], in0=ut[n][:, t, :], scalar1=ph, scalar2=None, op0=ALU.add)

        def reduce(n):
            c, g = UNITS[n]
            u, k = ut[n], kt.pop(n)
            for t in range(4):
                nc.vector.scalar_tensor_tensor(
                    out=u[:, t, :], in0=u[:, t, :], scalar=phi[:, 4 * g + t : 4 * g + t + 1], in1=k[:, t, :], op0=ALU.add, op1=ALU.subtract
                )

        def trig(n):
            c, g = UNITS[n]
            w = width(n)
            f = ut.pop(n)
            s = work.tile([P, 4, w], F32, name="s", tag="s", bufs=B_S)
            nc.scalar.activation(out=s[:], in_=f[:], func=AF.Sin, scale=TWO_PI)
            nc.scalar.activation(out=f[:], in_=f[:], func=AF.Abs)
            nc.scalar.activation(out=f[:], in_=f[:], func=AF.Sin, scale=-TWO_PI, bias=halfpi[:])
            trig_t[n] = [f, s]
            for i, name, bufs in ((1, "sb", B_SB), (0, "cb", B_CB)):
                if n in AMP_ACT[1 - i]:
                    src = trig_t[n][i]
                    trig_t[n][i] = work.tile([P, 4, w], BF16, name=name, tag=name, bufs=bufs, align_bytes=64)
                    for t in range(4):
                        nc.scalar.activation(out=trig_t[n][i][:, t, :], in_=src[:, t, :], func=AF.Copy, scale=ampf[:, 4 * g + t : 4 * g + t + 1])

        def group(n, i):
            if n not in grp_t:
                grp_t[n] = work.tile([P, 2, 4 * width(n)], BF16, name="grp", tag="grp", bufs=N_GRP, align_bytes=64)
            return grp_t[n][:, i, :]

        def features(n):
            c, g = UNITS[n]
            w = width(n)
            for i in range(2):
                src = trig_t[n][i]
                r = 4 if n in AMP_ACT[1 - i] else 2
                dst = group(n, i).rearrange("p (c i t) -> p c t i", i=r, t=4)
                src = src[:].rearrange("p t (c i) -> p c t i", i=r)
                if r == 4:
                    nc.vector.tensor_copy(out=dst, in_=src)
                else:
                    am = pa_t[:, 32 + 4 * g : 36 + 4 * g].unsqueeze(1).unsqueeze(3).to_broadcast([P, w // 2, 4, 2])
                    nc.vector.tensor_tensor(out=dst, in0=src, in1=am, op=ALU.mult)

        def feat_quant(n):
            mxq(
                f_codes[UNITS[n]][:].rearrange("p i w -> p (i w)"),
                f_scales[UNITS[n]][:].rearrange("p i w -> p (i w)"),
                grp_t.pop(n)[:].rearrange("p i w -> p (i w)"),
                E5,
            )

        acc = {}

        def stage2(c, mt, gs):
            rows = slice(P * mt, P * (mt + 1))
            if (c, mt) not in acc:
                re_ = psa.tile([P, C], F32, name="re", tag="acc")
                im_ = psa.tile([P, C], F32, name="im", tag="acc")
                acc[c, mt] = (re_, im_)
            re_, im_ = acc[c, mt]
            for g in gs:
                for i, pair in ((0, ((re_, 0), (im_, 2))), (1, ((re_, 1), (im_, 0)))):
                    for o, w in pair:
                        nc.tensor.matmul_mx(
                            out=o[:],
                            lhsT=f_codes[c, g][:, i, rows].bitcast(E5),
                            lhsT_scale=f_scales[c, g][:, i, rows],
                            rhs=w_side(w_codes, w, g).bitcast(E4),
                            rhs_scale=w_side(w_scales, w, g),
                            start=(g == 0 and i == 0),
                            stop=(g == G - 1 and i == 1),
                        )

        def finish(c, mt):
            r0 = CHUNKS[c][0] + P * mt
            for i, (o, dst) in enumerate(zip(acc.pop((c, mt)), (out_re, out_im))):
                r = work.tile([P, C], F32, name="r", tag="r", bufs=4)
                nc.vector.tensor_tensor(out=r[:], in0=o[:], in1=off[:, C * i : C * (i + 1)], op=ALU.add)
                nc.sync.dma_start(out=dst[r0 : r0 + P, :], in_=r[:])

        o_lay(0, 0, "v", (0, 3))
        o_lay(0, 0, "s", (3, 4))
        nc.vector.tensor_scalar(out=phi[:], in0=pa_t[:, 0 : 4 * G], scalar1=1.0 / TWO_PI, scalar2=None, op0=ALU.mult)
        nc.vector.tensor_copy(out=ampf[:], in_=pa_t[:, 32 : 32 + 4 * G])
        o_quant(0, 0)
        o_lay(0, 1, "v", (0, 2))
        x_quant(0)
        o_quant(0, 1, (0, 2))
        o_lay(0, 1, "s", (2, 4))
        stage1(0, [0])
        turns(0, [0])
        o_quant(0, 1, (2, 4))
        stage1(0, [1])
        x_turn(1)
        ofp = spread(of_t)
        nc.scalar.copy(out=off[:], in_=ofp[:])
        load_x(2)
        x_turn(2)

        dve_lay = {0: [("o", 1, 0), ("o", 1, 1)], 1: [("o", 2, 0)]}
        act_lay = {0: [("o", 2, 1)], 1: [(0, 0), (1, 0)], 2: [(0, 1), (1, 1), (0, 2)], 3: [(1, 2)]}
        early = {0: [("x", 1), ("x", 2)]}
        late = {
            0: [("o", 1, 0), ("o", 1, 1)], 1: [("o", 2, 0), ("o", 2, 1)], 2: [("w", 0, 0), ("w", 1, 0)], 3: [("w", 0, 1), ("w", 1, 1)], 4: [("x", 3), ("w", 0, 2), ("w", 1, 2)],
        }
        turn = {3: 3}
        ALL = (0, 1, 2)
        mm2 = {
            6: [(1, 0, ALL)], 7: [(1, 1, ALL), (1, 2, ALL)], 8: [(1, 3, ALL), (0, 0, ALL)], 9: [(0, 1, ALL)],
            10: [(2, 0, (0,)), (2, 1, (0,)), (2, 0, (1,)), (2, 1, (1,))], 11: [(2, 0, (2,)), (2, 1, (2,))],
        }
        fin = {7: [(1, 0)], 8: [(1, 1), (1, 2)], 9: [(1, 3), (0, 0)], 10: [(0, 1)], 12: [(2, 0), (2, 1)]}

        def do_quants(tasks):
            for task in tasks:
                if task[0] == "x":
                    x_quant(task[1])
                elif task[0] == "o":
                    o_quant(task[1], task[2])
                else:
                    w_quant(task[1], task[2])

        def lay(tasks, engine):
            for task in tasks:
                if task[0] == "o":
                    o_lay(task[1], task[2], engine)
                else:
                    w_lay(task[0], task[1], engine)

        for n in range(NU + 4):
            last = n >= NU
            if n == 0:
                turns(0, [1])
            elif n < NU:
                turns(n)
            for c, mt in fin.get(n, []):
                finish(c, mt)
            if 0 <= n - 1 < NU:
                nearest(n - 1, True, last)
            if n == NU:
                reduce(n - 1)
                trig(n - 1)
            do_quants(early.get(n, []))
            if n in turn:
                x_turn(turn[n])
            lay(dve_lay.get(n, []), "v")
            do_quants(late.get(n, []))
            if n + 1 < NU:
                stage1(n + 1)
            if 0 <= n - 1 < NU and not last:
                nearest(n - 1, False, True)
            if 0 <= n - 3 < NU:
                features(n - 3)
            if 0 <= n - 1 < NU and not last:
                reduce(n - 1)
                trig(n - 1)
            lay(act_lay.get(n, []), "s")
            for f, args in late_load.get(n, []):
                f(*args)
            if 0 <= n - 3 < NU:
                feat_quant(n - 3)
            for c, mt, gs in mm2.get(n, []):
                stage2(c, mt, gs)
